import numpy as np
import ml_dtypes


def mxq(x, axis, fmt="e4m3"):
    dtype, down = {"e4m3": (ml_dtypes.float8_e4m3fn, 7), "e5m2": (ml_dtypes.float8_e5m2, 14)}[fmt]
    v = np.moveaxis(np.asarray(x, np.float32).astype(ml_dtypes.bfloat16).astype(np.float64), axis, -1)
    blocks = v.reshape(v.shape[:-1] + (-1, 32))
    amax = np.abs(blocks).max(-1, keepdims=True)
    byte = np.maximum(np.where(amax > 0, np.frexp(amax)[1] - 1 + 127, 0) - down, 1)
    scale = np.exp2(byte - 127.0)
    codes = (blocks / scale).astype(np.float32).astype(dtype).astype(np.float64)
    return np.moveaxis((codes * scale).reshape(v.shape), -1, axis)


WIDE = False


def mx_kscale(k):
    if not WIDE:
        return np.ones(k)
    levels = np.array([10, -10, 5, -5, 0])
    if k % 512:
        return np.exp2(np.random.permutation(np.resize(levels, k // 32))).repeat(32)
    a = np.empty((k // 512, 16))
    for p in range(k // 512):
        a[p, :8] = np.random.permutation(np.resize(levels, 8))
        for g in range(8):
            far = levels[np.abs(levels - a[p, g]) >= 10]
            a[p, g + 8] = far[np.random.randint(len(far))]
    return np.exp2(a.ravel()).repeat(32)


BF16 = ml_dtypes.bfloat16


def bf(x):
    return np.asarray(x, np.float32).astype(BF16)


def f64(x):
    return np.asarray(x).astype(np.float64)


E2M1 = np.array([0.0, 0.5, 1.0, 1.5, 2.0, 3.0, 4.0, 6.0, -0.0, -0.5, -1.0, -1.5, -2.0, -3.0, -4.0, -6.0])


def pack_weight(w, fmt):
    k, n = w.shape
    w = f64(bf(w)).reshape(k // 32, 32, n)
    amax = np.abs(w).max(1)
    if fmt == "e4m3":
        byte = np.frexp(amax)[1] - 1 + 127 - 7
    else:
        mant, ex = np.frexp(amax / 6.0)
        byte = np.where(mant > 0.5, ex, ex - 1) + 127
    byte = np.clip(np.where(amax > 0, byte, 1), 1, 254)
    scaled = (w * np.exp2(127.0 - byte)[:, None, :]).reshape(k, n).astype(np.float32)
    by_word = np.ascontiguousarray(scaled.reshape(k // 512, 128, 4, n).transpose(0, 1, 3, 2))
    if fmt == "e4m3":
        words = by_word.astype(ml_dtypes.float8_e4m3fn).view(np.uint8)
    else:
        c = by_word.astype(ml_dtypes.float4_e2m1fn).view(np.uint8) & 0xF
        words = c[..., 0::2] | (c[..., 1::2] << 4)
    return np.ascontiguousarray(words), np.ascontiguousarray(byte.astype(np.uint8).reshape(k // 512, 16, n))


def unpack_weight(words, scales, fmt):
    g, p, n, _ = words.shape
    if fmt == "e4m3":
        vals = np.ascontiguousarray(words).view(ml_dtypes.float8_e4m3fn).astype(np.float64)
    else:
        nib = np.empty((g, p, n, 4), np.uint8)
        nib[..., 0::2] = words & 0xF
        nib[..., 1::2] = words >> 4
        vals = E2M1[nib]
    vals = vals * np.repeat(np.exp2(scales.astype(np.float64) - 127.0), 8, axis=1)[..., None]
    return vals.transpose(0, 1, 3, 2).reshape(g * 512, n)
def pack4(w):
    words, scales = pack_weight(w, "e2m1")
    return words.reshape(words.shape[0], 128, -1), scales


def unpack4(words, scales):
    return unpack_weight(words.reshape(words.shape[0], 128, -1, 2), scales, "e2m1")


def planes(Y):
    n, m = Y.shape
    b = f64(bf(Y)).reshape(n // 32, 32, m)
    amax = np.abs(b).max(1)
    byte = np.clip(np.where(amax > 0, np.frexp(amax)[1] - 1 + 127 - 7, 1), 1, 254)
    codes = (b * np.exp2(127.0 - byte)[:, None, :]).reshape(n, m).astype(np.float32).astype(ml_dtypes.float8_e4m3fn).view(np.uint8)
    words = codes.reshape(n // 512, 128, 4, m).transpose(0, 1, 3, 2)
    return np.ascontiguousarray(words), np.ascontiguousarray(byte.astype(np.uint8).reshape(n // 512, 16, m))


T, B, B2, F, F2 = 1024, 1024, 2048, 512, 1024
NORM = 0.75

def real_form(re, im):
    return np.block([[re, im], [-im, re]])

def setup_inputs():
    s, t = mx_kscale(B2), mx_kscale(F2)
    currents = np.random.randn(T, B2)
    u = np.random.uniform(-1.0, 1.0, B)
    phase = np.pi * u[:, None] * (np.arange(F) - (F - 1) / 2)[None, :]
    steering = real_form(np.cos(phase), np.sin(phase)) / np.sqrt(B)
    taper = 1 + 0.1 * np.random.randn(F)
    conj_taper = np.concatenate([taper, -taper])
    cr, ci = np.random.randn(F, F), np.random.randn(F, F)
    coupling = real_form(cr + cr.T, ci + ci.T) / np.sqrt(F + F)
    excitation = np.exp(0.8 * np.random.randn(F))[None, :] * np.exp(0.3 * np.random.randn(T, F))
    steering_words, steering_scales = pack4(steering / s[:, None])
    coupling_words, coupling_scales = pack4(coupling / t[:, None])
    return {"currents": bf(currents * s[None, :]),
            "steering_words": steering_words, "steering_scales": steering_scales,
            "conj_taper": bf(conj_taper * t),
            "coupling_words": coupling_words, "coupling_scales": coupling_scales,
            "excitation": bf(excitation)}

def reference(currents, steering_words, steering_scales, conj_taper, coupling_words, coupling_scales, excitation):
    S = unpack4(steering_words, steering_scales)
    C = unpack4(coupling_words, coupling_scales)
    h = (mxq(f64(currents), 1, "e4m3") @ S) * f64(conj_taper)[None, :]
    v = (mxq(h, 1, "e4m3") @ C) * NORM
    y = (v.reshape(T, -1, F) * f64(excitation)[:, None, :]).reshape(T, F2)
    Y = y.T
    words, scales = planes(Y)
    return y, words, scales

@@ -1,0 +1,328 @@
+from contextlib import ExitStack
+
+import concourse.mybir as mybir
+from concourse.masks import make_identity
+
+T, K1, F2, F = 1024, 2048, 1024, 512
+NORM = 0.75
+FLOPS = 2 * T * K1 * F2 + 2 * T * F2 * F2
+
+F32 = mybir.dt.float32
+BF16 = mybir.dt.bfloat16
+I32 = mybir.dt.int32
+U32 = mybir.dt.uint32
+U8 = mybir.dt.uint8
+FP8X4 = mybir.dt.float8_e4m3fn_x4
+FP4X4 = mybir.dt.float4_e2m1fn_x4
+MULT = mybir.AluOpType.mult
+
+P = 128
+BANK = 512
+TILES = T // P
+G1 = K1 // 512
+G2 = F2 // 512
+WORD_GROUPS = ((0, 4), (4, 6), (6, 7), (7, 8))
+SCALE_GROUPS = ((0, 6), (6, 8))
+
+
+def tile_array_excitation_product_h1_kernel(
+    tc, currents, steering_words, steering_scales, conj_taper, coupling_words, coupling_scales, excitation,
+    out_0, out_1, out_2,
+):
+    nc = tc.nc
+    with ExitStack() as ctx:
+        keep = ctx.enter_context(tc.tile_pool(name="keep", bufs=1))
+        work = ctx.enter_context(tc.tile_pool(name="work", bufs=3))
+        psum = ctx.enter_context(tc.psum_pool(name="psum", bufs=1))
+        ctx.enter_context(tc.manual_schedule())
+
+        def bank(tag):
+            return psum.tile([P, BANK], F32, name=tag, tag=tag)
+
+        def kept(name, shape, dtype):
+            return keep.tile(shape, dtype, name=name, tag=name, align_bytes=64)
+
+        def rotating(tag, shape, dtype):
+            return work.tile(shape, dtype, name=tag, tag=tag, align_bytes=64)
+
+        def load_scale_rows(plane, scales, passes):
+            rows = scales.bitcast(I32).rearrange("g (q r) n -> r q g n", r=4)
+            for r in range(4):
+                nc.sync.dma_start(
+                    out=plane[r:P:32, :].bitcast(I32).rearrange("q (g n) -> q g n", g=passes), in_=rows[r])
+
+        s_scale = kept("s_scale", [P, G1 * F2], U8)
+        c_scale = kept("c_scale", [P, G2 * F2], U8)
+        nc.vector.memset(s_scale[:].bitcast(I32), 0)
+        ident = kept("ident", [P, P], F32)
+        make_identity(nc, ident[:])
+        nc.vector.memset(c_scale[:].bitcast(I32), 0)
+
+        half = K1 // 2
+        x_first = [kept("x_first%d" % h, [P, half], BF16) for h in range(2)]
+        x_raw = [None] + [kept("x_raw%d" % s, [P, K1], BF16) for s in range(1, TILES)]
+        s_words = [kept("s_words%d" % g, [P, 2 * F2], U8) for g in range(G1)]
+        c_words = kept("c_words", [P, G2 * 2 * F2], U8)
+        exc = [kept("exc%d" % h, [P, TILES // 2, F], BF16) for h in range(2)]
+        taper_col = kept("taper_col", [P, G2 * 4], BF16)
+        taper = kept("taper", [P, F2], BF16)
+
+        def load_x(s):
+            nc.sync.dma_start(out=x_raw[s][:], in_=currents[s * P:(s + 1) * P, :])
+
+        def load_s(g):
+            nc.sync.dma_start(out=s_words[g][:].bitcast(I32), in_=steering_words[g].bitcast(I32))
+
+        def load_exc(h):
+            rows = excitation[h * T // 2:(h + 1) * T // 2, :]
+            nc.sync.dma_start(out=exc[h][:], in_=rows.rearrange("(s p) j -> p s j", p=P))
+
+        nc.sync.dma_start(out=x_first[0][:], in_=currents[0:P, 0:half])
+        nc.sync.dma_start(
+            out=taper_col[:].rearrange("p (g t) -> p g t", t=4),
+            in_=conj_taper.rearrange("(g p t) -> p g t", p=P, t=4))
+        load_scale_rows(s_scale, steering_scales, G1)
+        load_s(0)
+        nc.sync.dma_start(out=x_first[1][:], in_=currents[0:P, half:K1])
+        for g in range(1, G1):
+            load_s(g)
+        load_x(1)
+        load_x(2)
+        load_scale_rows(c_scale, coupling_scales, G2)
+        nc.sync.dma_start(
+            out=c_words[:].bitcast(I32).rearrange("p (g n) -> p g n", g=G2),
+            in_=coupling_words.bitcast(I32).rearrange("g p n -> p g n"))
+        load_exc(0)
+        load_x(3)
+        load_x(4)
+        load_x(5)
+        load_exc(1)
+        load_x(6)
+        load_x(7)
+
+        y_words = {}
+        for lo, hi in WORD_GROUPS:
+            group = kept("y_words%d" % lo, [P, G2, (hi - lo) * P], U32)
+            for s in range(lo, hi):
+                y_words[s] = (group, lo, hi)
+        y_scale = {}
+        for lo, hi in SCALE_GROUPS:
+            group = kept("y_scale%d" % lo, [P, G2, (hi - lo) * P], U8)
+            for s in range(lo, hi):
+                y_scale[s] = (group, lo, hi)
+
+        x_sorted, x_codes, h_bank, h_pairs, h_codes = {}, {}, {}, {}, {}
+        y_bank, y_f32, y_pairs, y_grouped = {}, {}, {}, {}
+
+        def sort_x(s, h):
+            dst = rotating("x_sorted%d" % h, [P, BANK], F32)
+            src = x_raw[s][:].bitcast(F32)[:, h * BANK:(h + 1) * BANK]
+            out = dst[:].rearrange("p (u c i) -> p c u i", u=2, i=4)
+            in_ = src.rearrange("p (c i u) -> p c u i", u=2, i=4)
+            if h == 0:
+                nc.vector.tensor_copy(out=out, in_=in_)
+            else:
+                nc.scalar.copy(out=out, in_=in_)
+            x_sorted[s, h] = dst
+
+        def turn(dst, slot, words):
+            nc.tensor.transpose(dst[:, slot * P:(slot + 1) * P], words, ident[:])
+
+        def turn_x(s, h):
+            dst = bank("xt%d" % h)
+            for g in range(2):
+                for u in range(2):
+                    start = u * 2 * P + g * P
+                    turn(dst, 2 * g + u, x_sorted[s, h][:, start:start + P])
+            return dst
+
+        def turn_pairs(dst, first_slot, pairs):
+            words = pairs[:].bitcast(F32)
+            for u in range(2):
+                turn(dst, first_slot + u, words[:, u * P:(u + 1) * P])
+
+        def group_words(engine_copy, tag, src, passes):
+            dst = rotating(tag, [P, passes * BANK], BF16)
+            engine_copy(
+                out=dst[:].bitcast(F32).rearrange("p (g r u) -> p g r u", g=passes, u=2),
+                in_=src[:, 0:passes * 2 * P].rearrange("p (g u r) -> p g r u", g=passes, u=2))
+            return dst
+
+        def quantize(tag, grouped, passes):
+            codes = rotating(tag + "_codes", [P, passes * P], U32)
+            scales = rotating(tag + "_scales", [P, passes * P], U8)
+            nc.vector.quantize_mx(out=codes[:].bitcast(FP8X4), scales=scales[:], in_=grouped[:])
+            return [(codes[:, g * P:(g + 1) * P], scales[:, g * P:(g + 1) * P]) for g in range(passes)]
+
+        def mx_pass(acc, stationary, words, scale, n, first, last):
+            codes, scales = stationary
+            nc.tensor.matmul_mx(
+                out=acc[:],
+                lhsT=codes.bitcast(FP8X4), lhsT_scale=scales,
+                rhs=words[:, n * 2 * BANK:(n + 1) * 2 * BANK].bitcast(FP4X4),
+                rhs_scale=scale[:, n * BANK:(n + 1) * BANK],
+                start=first, stop=last)
+
+        def stage1_pass(s, n, g):
+            if g == 0:
+                h_bank[s, n] = bank("h%d" % n)
+            mx_pass(h_bank[s, n], x_codes[s][g], s_words[g][:], s_scale[:, g * F2:(g + 1) * F2], n,
+                    g == 0, g == G1 - 1)
+
+        def stage2(s, tags):
+            for n in range(2):
+                y_bank[s, n] = bank(tags[n])
+                for g in range(G2):
+                    mx_pass(y_bank[s, n], h_codes[s][g], c_words[:, g * 2 * F2:(g + 1) * 2 * F2],
+                            c_scale[:, g * F2:(g + 1) * F2], n, g == 0, g == G2 - 1)
+
+        def taper_h(s, n):
+            dst = rotating("h_pairs%d" % n, [P, BANK], BF16)
+            nc.vector.tensor_tensor(
+                out=dst[:].rearrange("p (u w e) -> p u w e", u=2, e=2),
+                in0=h_bank[s, n][:].rearrange("p (w u e) -> p u w e", u=2, e=2),
+                in1=taper[:, n * BANK:(n + 1) * BANK].rearrange("p (u w e) -> p u w e", u=2, e=2),
+                op=MULT)
+            h_pairs[s, n] = dst
+
+        def excite(s, n):
+            if n == 0:
+                y_f32[s] = rotating("y_f32", [P, F2], F32)
+            nc.vector.scalar_tensor_tensor(
+                out=y_f32[s][:, n * BANK:(n + 1) * BANK], in0=y_bank[s, n][:], scalar=NORM,
+                in1=exc[s // (TILES // 2)][:, s % (TILES // 2), :], op0=MULT, op1=MULT)
+
+        def round_y(s, n):
+            dst = rotating("y_pairs%d" % n, [P, BANK], BF16)
+            nc.scalar.copy(
+                out=dst[:].rearrange("p (u w e) -> p u w e", u=2, e=2),
+                in_=y_f32[s][:, n * BANK:(n + 1) * BANK].rearrange("p (w u e) -> p u w e", u=2, e=2))
+            y_pairs[s, n] = dst
+
+        def quantize_y(s, n, grouped):
+            words, wlo, whi = y_words[s]
+            scales, slo, shi = y_scale[s]
+            nc.vector.quantize_mx(
+                out=words[:, n, (s - wlo) * P:(s - wlo + 1) * P].bitcast(FP8X4),
+                scales=scales[:, n, (s - slo) * P:(s - slo + 1) * P],
+                in_=grouped)
+
+        def store_y(s, lo, hi):
+            nc.sync.dma_start(out=out_0[s * P:(s + 1) * P, lo:hi], in_=y_f32[s][:, lo:hi])
+
+        def store_planes(s):
+            words, wlo, whi = y_words[s]
+            if s == whi - 1:
+                dst = out_1.rearrange("g p m t -> p g (m t)").bitcast(I32)
+                nc.sync.dma_start(out=dst[:, :, wlo * P:whi * P], in_=words[:].bitcast(I32))
+            scales, slo, shi = y_scale[s]
+            if s == shi - 1:
+                dst = out_2.bitcast(I32).rearrange("g q m -> q g m")
+                for q in range(4):
+                    queue = nc.scalar if (s == TILES - 1 and q % 2 == 1) else nc.sync
+                    queue.dma_start(
+                        out=dst[4 * q:4 * q + 4, :, slo * P // 4:shi * P // 4],
+                        in_=scales[32 * q:32 * q + 4, :, :].bitcast(I32))
+
+        first_tags = ("xt0", "xt1", "ht", "y0")
+        x_codes[0] = []
+        for g in range(G1):
+            dst = bank(first_tags[g])
+            words = x_first[g // 2][:].bitcast(F32)
+            for u in range(2):
+                base = (g % 2) * 2 * P
+                turn(dst, u, words[:, base + u:base + 2 * P:2])
+            grouped = group_words(nc.scalar.copy, "x_first_grouped", dst, 1)
+            x_codes[0].extend(quantize("x_first%d" % g, grouped, 1))
+            if g == 1:
+                spread = bank("yt")
+                for slot in range(4):
+                    turn(spread, slot, taper_col[:].bitcast(F32)[:, slot:slot + 1].to_broadcast([P, P]))
+        nc.scalar.copy(out=taper[:].bitcast(F32), in_=spread[:])
+        for g in range(G1):
+            for n in range(2):
+                stage1_pass(0, n, g)
+        sort_x(1, 0)
+        sort_x(1, 1)
+        taper_h(0, 0)
+
+        for s in range(1, TILES):
+            xt = [turn_x(s, h) for h in range(2)]
+            taper_h(s - 1, 1)
+            if s >= 3:
+                yt = bank("yt")
+                for n in range(2):
+                    turn_pairs(yt, 2 * n, y_pairs[s - 3, n])
+            ht = bank("ht")
+            for n in range(2):
+                turn_pairs(ht, 2 * n, h_pairs[s - 1, n])
+            x_grouped = [group_words(nc.scalar.copy, "x_grouped%d" % h, xt[h], 2) for h in range(2)]
+            h_grouped = group_words(nc.scalar.copy, "h_grouped", ht, 2)
+            if s >= 3:
+                y_grouped = group_words(nc.scalar.copy, "y_grouped", yt, 2)
+            if s + 1 < TILES:
+                sort_x(s + 1, 0)
+            x_codes[s] = quantize("x0", x_grouped[0], 2) + quantize("x1", x_grouped[1], 2)
+            if s >= 2:
+                stage2(s - 2, ("y0", "y1"))
+                excite(s - 2, 0)
+                round_y(s - 2, 0)
+            h_codes[s - 1] = quantize("h", h_grouped, 2)
+            if s + 1 < TILES:
+                sort_x(s + 1, 1)
+            if s >= 2:
+                excite(s - 2, 1)
+                round_y(s - 2, 1)
+                store_y(s - 2, 0, F2)
+            if s >= 3:
+                for n in range(2):
+                    quantize_y(s - 3, n, y_grouped[:, n * BANK:(n + 1) * BANK])
+                store_planes(s - 3)
+            for n in range(2):
+                for g in range(G1):
+                    stage1_pass(s, n, g)
+                if n == 0:
+                    taper_h(s, 0)
+
+        last = TILES - 1
+        taper_h(last, 1)
+        yt = bank("yt")
+        for n in range(2):
+            turn_pairs(yt, 2 * n, y_pairs[last - 2, n])
+        ht = bank("ht")
+        for n in range(2):
+            turn_pairs(ht, 2 * n, h_pairs[last, n])
+        h_grouped = group_words(nc.scalar.copy, "h_grouped", ht, 2)
+        y_grouped = group_words(nc.scalar.copy, "y_grouped", yt, 2)
+        stage2(last - 1, ("y0", "y1"))
+        h_codes[last] = quantize("h", h_grouped, 2)
+        stage2(last, ("h0", "h1"))
+        excite(last - 1, 0)
+        round_y(last - 1, 0)
+        excite(last - 1, 1)
+        round_y(last - 1, 1)
+        store_y(last - 1, 0, F2)
+        excite(last, 0)
+        round_y(last, 0)
+        store_y(last, 0, BANK)
+        excite(last, 1)
+        round_y(last, 1)
+        store_y(last, BANK, F2)
+        for n in range(2):
+            quantize_y(last - 2, n, y_grouped[:, n * BANK:(n + 1) * BANK])
+        store_planes(last - 2)
+        yt = bank("xt0")
+        for n in range(2):
+            turn_pairs(yt, 2 * n, y_pairs[last - 1, n])
+        y_grouped = group_words(nc.vector.tensor_copy, "y_grouped", yt, 2)
+        tail = []
+        for n in range(2):
+            yt = bank(("xt1", "ht")[n])
+            turn_pairs(yt, 0, y_pairs[last, n])
+            tail.append(group_words(nc.scalar.copy, "y_last%d" % n, yt, 1))
+        for n in range(2):
+            quantize_y(last - 1, n, y_grouped[:, n * BANK:(n + 1) * BANK])
+        store_planes(last - 1)
+        for n in range(2):
+            quantize_y(last, n, tail[n][:])
+        store_planes(last)

@@ -21,8 +21,8 @@ BANK = 512
 TILES = T // P
 G1 = K1 // 512
 G2 = F2 // 512
-WORD_GROUPS = ((0, 4), (4, 6), (6, 7), (7, 8))
-SCALE_GROUPS = ((0, 6), (6, 8))
+WORD_GROUPS = ((0, 3), (3, 5), (5, 7), (7, 8))
+SCALE_GROUPS = ((0, 5), (5, 8))
 
 
 def tile_array_excitation_product_h1_kernel(
@@ -54,6 +54,10 @@ def tile_array_excitation_product_h1_kernel(
         s_scale = kept("s_scale", [P, G1 * F2], U8)
         c_scale = kept("c_scale", [P, G2 * F2], U8)
         nc.vector.memset(s_scale[:].bitcast(I32), 0)
+        taper_col = kept("taper_col", [P, G2 * 4], BF16)
+        nc.scalar.dma_start(
+            out=taper_col[:].rearrange("p (g t) -> p g t", t=4),
+            in_=conj_taper.rearrange("(g p t) -> p g t", p=P, t=4))
         ident = kept("ident", [P, P], F32)
         make_identity(nc, ident[:])
         nc.vector.memset(c_scale[:].bitcast(I32), 0)
@@ -64,7 +68,6 @@ def tile_array_excitation_product_h1_kernel(
         s_words = [kept("s_words%d" % g, [P, 2 * F2], U8) for g in range(G1)]
         c_words = kept("c_words", [P, G2 * 2 * F2], U8)
         exc = [kept("exc%d" % h, [P, TILES // 2, F], BF16) for h in range(2)]
-        taper_col = kept("taper_col", [P, G2 * 4], BF16)
         taper = kept("taper", [P, F2], BF16)
 
         def load_x(s):
@@ -78,22 +81,20 @@ def tile_array_excitation_product_h1_kernel(
             nc.sync.dma_start(out=exc[h][:], in_=rows.rearrange("(s p) j -> p s j", p=P))
 
         nc.sync.dma_start(out=x_first[0][:], in_=currents[0:P, 0:half])
-        nc.sync.dma_start(
-            out=taper_col[:].rearrange("p (g t) -> p g t", t=4),
-            in_=conj_taper.rearrange("(g p t) -> p g t", p=P, t=4))
+        nc.sync.dma_start(out=x_first[1][:], in_=currents[0:P, half:K1])
         load_scale_rows(s_scale, steering_scales, G1)
         load_s(0)
-        nc.sync.dma_start(out=x_first[1][:], in_=currents[0:P, half:K1])
-        for g in range(1, G1):
-            load_s(g)
+        load_s(1)
         load_x(1)
+        load_s(2)
+        load_s(3)
         load_x(2)
         load_scale_rows(c_scale, coupling_scales, G2)
         nc.sync.dma_start(
             out=c_words[:].bitcast(I32).rearrange("p (g n) -> p g n", g=G2),
             in_=coupling_words.bitcast(I32).rearrange("g p n -> p g n"))
-        load_exc(0)
         load_x(3)
+        load_exc(0)
         load_x(4)
         load_x(5)
         load_exc(1)
@@ -116,10 +117,13 @@ def tile_array_excitation_product_h1_kernel(
 
         def sort_x(s, h):
             dst = rotating("x_sorted%d" % h, [P, BANK], F32)
-            src = x_raw[s][:].bitcast(F32)[:, h * BANK:(h + 1) * BANK]
+            if s == 0:
+                src = x_first[h][:].bitcast(F32)
+            else:
+                src = x_raw[s][:].bitcast(F32)[:, h * BANK:(h + 1) * BANK]
             out = dst[:].rearrange("p (u c i) -> p c u i", u=2, i=4)
             in_ = src.rearrange("p (c i u) -> p c u i", u=2, i=4)
-            if h == 0:
+            if s <= 1 or (h == 0 and s > 2):
                 nc.vector.tensor_copy(out=out, in_=in_)
             else:
                 nc.scalar.copy(out=out, in_=in_)
@@ -165,16 +169,24 @@ def tile_array_excitation_product_h1_kernel(
 
         def stage1_pass(s, n, g):
             if g == 0:
-                h_bank[s, n] = bank("h%d" % n)
+                h_bank[s, n] = bank(("y%d" if s == 0 else "h%d") % n)
             mx_pass(h_bank[s, n], x_codes[s][g], s_words[g][:], s_scale[:, g * F2:(g + 1) * F2], n,
                     g == 0, g == G1 - 1)
 
-        def stage2(s, tags):
+        def stage1(s, n):
+            for g in range(G1):
+                stage1_pass(s, n, g)
+
+        def stage2_pass(s, n, g):
+            if g == 0:
+                y_bank[s, n] = bank(("h%d" if s == TILES - 1 else "y%d") % n)
+            mx_pass(y_bank[s, n], h_codes[s][g], c_words[:, g * 2 * F2:(g + 1) * 2 * F2],
+                    c_scale[:, g * F2:(g + 1) * F2], n, g == 0, g == G2 - 1)
+
+        def stage2(s):
             for n in range(2):
-                y_bank[s, n] = bank(tags[n])
                 for g in range(G2):
-                    mx_pass(y_bank[s, n], h_codes[s][g], c_words[:, g * 2 * F2:(g + 1) * 2 * F2],
-                            c_scale[:, g * F2:(g + 1) * F2], n, g == 0, g == G2 - 1)
+                    stage2_pass(s, n, g)
 
         def taper_h(s, n):
             dst = rotating("h_pairs%d" % n, [P, BANK], BF16)
@@ -197,6 +209,18 @@ def tile_array_excitation_product_h1_kernel(
             nc.scalar.copy(
                 out=dst[:].rearrange("p (u w e) -> p u w e", u=2, e=2),
                 in_=y_f32[s][:, n * BANK:(n + 1) * BANK].rearrange("p (w u e) -> p u w e", u=2, e=2))
+            y_pairs[s, n] = dst
+
+        def excite_pairs(s, n):
+            dst = rotating("y_pairs%d" % n, [P, BANK], BF16)
+            factor = exc[s // (TILES // 2)][:, s % (TILES // 2), :]
+            for u in range(2):
+                nc.vector.scalar_tensor_tensor(
+                    out=dst[:, u * 2 * P:(u + 1) * 2 * P].rearrange("p (w e) -> p w e", e=2),
+                    in0=y_bank[s, n][:].rearrange("p (w u e) -> p u w e", u=2, e=2)[:, u],
+                    scalar=NORM,
+                    in1=factor.rearrange("p (w u e) -> p u w e", u=2, e=2)[:, u],
+                    op0=MULT, op1=MULT)
             y_pairs[s, n] = dst
 
         def quantize_y(s, n, grouped):
@@ -224,105 +248,132 @@ def tile_array_excitation_product_h1_kernel(
                         out=dst[4 * q:4 * q + 4, :, slo * P // 4:shi * P // 4],
                         in_=scales[32 * q:32 * q + 4, :, :].bitcast(I32))
 
-        first_tags = ("xt0", "xt1", "ht", "y0")
+        def turn_both(tag, pairs, s):
+            dst = bank(tag)
+            for n in range(2):
+                turn_pairs(dst, 2 * n, pairs[s, n])
+            return dst
+
+        first_tags = ("xt0", "xt1", "ht", "yt")
         x_codes[0] = []
-        for g in range(G1):
-            dst = bank(first_tags[g])
-            words = x_first[g // 2][:].bitcast(F32)
-            for u in range(2):
-                base = (g % 2) * 2 * P
-                turn(dst, u, words[:, base + u:base + 2 * P:2])
-            grouped = group_words(nc.scalar.copy, "x_first_grouped", dst, 1)
-            x_codes[0].extend(quantize("x_first%d" % g, grouped, 1))
-            if g == 1:
-                spread = bank("yt")
-                for slot in range(4):
-                    turn(spread, slot, taper_col[:].bitcast(F32)[:, slot:slot + 1].to_broadcast([P, P]))
-        nc.scalar.copy(out=taper[:].bitcast(F32), in_=spread[:])
-        for g in range(G1):
+
+        def first_half(h):
+            for g in range(2):
+                dst = bank(first_tags[2 * h + g])
+                for u in range(2):
+                    start = u * 2 * P + g * P
+                    turn(dst, u, x_sorted[0, h][:, start:start + P])
+                grouped = group_words(nc.scalar.copy, "x_first_grouped", dst, 1)
+                x_codes[0].extend(quantize("x_first%d" % (2 * h + g), grouped, 1))
+
+        def first_pass(g):
             for n in range(2):
                 stage1_pass(0, n, g)
+
+        spread = bank("h1")
+        for slot in range(4):
+            turn(spread, slot, taper_col[:].bitcast(F32)[:, slot:slot + 1].to_broadcast([P, P]))
+        nc.scalar.copy(out=taper[:].bitcast(F32), in_=spread[:])
+        sort_x(0, 0)
+        sort_x(0, 1)
+        first_half(0)
+        first_half(1)
+        first_pass(0)
+        first_pass(1)
         sort_x(1, 0)
         sort_x(1, 1)
+        xt = [turn_x(1, h) for h in range(2)]
+        x_grouped = [group_words(nc.scalar.copy, "x_grouped%d" % h, xt[h], 2) for h in range(2)]
+        x_codes[1] = quantize("x0", x_grouped[0], 2) + quantize("x1", x_grouped[1], 2)
+        for n in range(2):
+            for g in range(2, G1):
+                stage1_pass(0, n, g)
+        sort_x(2, 0)
+        sort_x(2, 1)
         taper_h(0, 0)
-
-        for s in range(1, TILES):
-            xt = [turn_x(s, h) for h in range(2)]
-            taper_h(s - 1, 1)
-            if s >= 3:
-                yt = bank("yt")
-                for n in range(2):
-                    turn_pairs(yt, 2 * n, y_pairs[s - 3, n])
-            ht = bank("ht")
-            for n in range(2):
-                turn_pairs(ht, 2 * n, h_pairs[s - 1, n])
-            x_grouped = [group_words(nc.scalar.copy, "x_grouped%d" % h, xt[h], 2) for h in range(2)]
-            h_grouped = group_words(nc.scalar.copy, "h_grouped", ht, 2)
-            if s >= 3:
-                y_grouped = group_words(nc.scalar.copy, "y_grouped", yt, 2)
-            if s + 1 < TILES:
-                sort_x(s + 1, 0)
-            x_codes[s] = quantize("x0", x_grouped[0], 2) + quantize("x1", x_grouped[1], 2)
-            if s >= 2:
-                stage2(s - 2, ("y0", "y1"))
-                excite(s - 2, 0)
-                round_y(s - 2, 0)
-            h_codes[s - 1] = quantize("h", h_grouped, 2)
-            if s + 1 < TILES:
-                sort_x(s + 1, 1)
-            if s >= 2:
-                excite(s - 2, 1)
-                round_y(s - 2, 1)
-                store_y(s - 2, 0, F2)
-            if s >= 3:
-                for n in range(2):
-                    quantize_y(s - 3, n, y_grouped[:, n * BANK:(n + 1) * BANK])
-                store_planes(s - 3)
-            for n in range(2):
-                for g in range(G1):
-                    stage1_pass(s, n, g)
-                if n == 0:
-                    taper_h(s, 0)
+        taper_h(0, 1)
+        stage1(1, 0)
 
         last = TILES - 1
-        taper_h(last, 1)
-        yt = bank("yt")
-        for n in range(2):
-            turn_pairs(yt, 2 * n, y_pairs[last - 2, n])
-        ht = bank("ht")
-        for n in range(2):
-            turn_pairs(ht, 2 * n, h_pairs[last, n])
+        for s in range(1, last):
+            ht = turn_both("ht", h_pairs, s - 1)
+            xt = [turn_x(s + 1, h) for h in range(2)]
+            if s >= 2:
+                yt = turn_both("yt", y_pairs, s - 2)
+            taper_h(s, 0)
+            h_grouped = group_words(nc.scalar.copy, "h_grouped", ht, 2)
+            if s < last:
+                x_grouped = [group_words(nc.scalar.copy, "x_grouped%d" % h, xt[h], 2) for h in range(2)]
+            if s >= 2:
+                y_grouped = group_words(nc.scalar.copy, "y_grouped", yt, 2)
+            if s + 2 < TILES:
+                sort_x(s + 2, 0)
+                sort_x(s + 2, 1)
+            h_codes[s - 1] = quantize("h", h_grouped, 2)
+            if s < last:
+                x_codes[s + 1] = quantize("x0", x_grouped[0], 2) + quantize("x1", x_grouped[1], 2)
+            stage1(s, 1)
+            taper_h(s, 1)
+            stage2(s - 1)
+            for n in range(2):
+                excite(s - 1, n)
+                round_y(s - 1, n)
+            store_y(s - 1, 0, F2)
+            if s >= 2:
+                for n in range(2):
+                    quantize_y(s - 2, n, y_grouped[:, n * BANK:(n + 1) * BANK])
+                store_planes(s - 2)
+            if s < last:
+                stage1(s + 1, 0)
+
+        def last_h(n):
+            ht = bank(("xt0", "xt1")[n])
+            turn_pairs(ht, 0, h_pairs[last, n])
+            return group_words(nc.scalar.copy, "h_last%d" % n, ht, 1)
+
+        def planes_of(s, grouped):
+            for n in range(2):
+                quantize_y(s, n, grouped[:, n * BANK:(n + 1) * BANK])
+            store_planes(s)
+
+        ht = turn_both("ht", h_pairs, last - 1)
+        taper_h(last, 0)
         h_grouped = group_words(nc.scalar.copy, "h_grouped", ht, 2)
-        y_grouped = group_words(nc.scalar.copy, "y_grouped", yt, 2)
-        stage2(last - 1, ("y0", "y1"))
-        h_codes[last] = quantize("h", h_grouped, 2)
-        stage2(last, ("h0", "h1"))
+        h_codes[last - 1] = quantize("h", h_grouped, 2)
+        stage1(last, 1)
+        taper_h(last, 1)
+        h_codes[last] = quantize("h_last0", last_h(0), 1)
+        for g in range(G2):
+            stage2_pass(last - 1, 0, g)
         excite(last - 1, 0)
+        grouped = last_h(1)
+        yt = turn_both("yt", y_pairs, last - 2)
+        h_codes[last].extend(quantize("h_last1", grouped, 1))
+        y_grouped = group_words(nc.scalar.copy, "y_grouped", yt, 2)
         round_y(last - 1, 0)
+        for g in range(G2):
+            stage2_pass(last - 1, 1, g)
+        for g in range(G2):
+            for n in range(2):
+                stage2_pass(last, n, g)
         excite(last - 1, 1)
         round_y(last - 1, 1)
         store_y(last - 1, 0, F2)
+        planes_of(last - 2, y_grouped)
         excite(last, 0)
         round_y(last, 0)
         store_y(last, 0, BANK)
+        excite_pairs(last, 1)
         excite(last, 1)
-        round_y(last, 1)
         store_y(last, BANK, F2)
-        for n in range(2):
-            quantize_y(last - 2, n, y_grouped[:, n * BANK:(n + 1) * BANK])
-        store_planes(last - 2)
-        yt = bank("xt0")
-        for n in range(2):
-            turn_pairs(yt, 2 * n, y_pairs[last - 1, n])
-        y_grouped = group_words(nc.vector.tensor_copy, "y_grouped", yt, 2)
-        tail = []
-        for n in range(2):
-            yt = bank(("xt1", "ht")[n])
+        yt = turn_both("yt", y_pairs, last - 1)
+        y_grouped = group_words(nc.scalar.copy, "y_grouped", yt, 2)
+        tail = {}
+        for n in (1, 0):
+            yt = bank(("xt0", "xt1")[n])
             turn_pairs(yt, 0, y_pairs[last, n])
-            tail.append(group_words(nc.scalar.copy, "y_last%d" % n, yt, 1))
-        for n in range(2):
-            quantize_y(last - 1, n, y_grouped[:, n * BANK:(n + 1) * BANK])
-        store_planes(last - 1)
-        for n in range(2):
+            tail[n] = group_words((nc.scalar.copy, nc.vector.tensor_copy)[n], "y_last%d" % n, yt, 1)
+        planes_of(last - 1, y_grouped)
+        for n in (1, 0):
             quantize_y(last, n, tail[n][:])
         store_planes(last)

@@ -211,6 +211,14 @@ def tile_array_excitation_product_h1_kernel(
                 in_=y_f32[s][:, n * BANK:(n + 1) * BANK].rearrange("p (w u e) -> p u w e", u=2, e=2))
             y_pairs[s, n] = dst
 
+        def round_tile(s):
+            dst = rotating("y_pairs", [P, F2], BF16)
+            nc.scalar.copy(
+                out=dst[:].rearrange("p (g u w e) -> p g u w e", g=G2, u=2, e=2),
+                in_=y_f32[s][:].rearrange("p (g w u e) -> p g u w e", g=G2, u=2, e=2))
+            for n in range(2):
+                y_pairs[s, n] = dst[:, n * BANK:(n + 1) * BANK]
+
         def excite_pairs(s, n):
             dst = rotating("y_pairs%d" % n, [P, BANK], BF16)
             factor = exc[s // (TILES // 2)][:, s % (TILES // 2), :]
@@ -255,16 +263,16 @@ def tile_array_excitation_product_h1_kernel(
             return dst
 
         first_tags = ("xt0", "xt1", "ht", "yt")
-        x_codes[0] = []
 
-        def first_half(h):
-            for g in range(2):
-                dst = bank(first_tags[2 * h + g])
+        def by_pass(s):
+            x_codes[s] = []
+            for g in range(G1):
+                dst = bank(first_tags[g])
                 for u in range(2):
-                    start = u * 2 * P + g * P
-                    turn(dst, u, x_sorted[0, h][:, start:start + P])
+                    start = u * 2 * P + (g % 2) * P
+                    turn(dst, u, x_sorted[s, g // 2][:, start:start + P])
                 grouped = group_words(nc.scalar.copy, "x_first_grouped", dst, 1)
-                x_codes[0].extend(quantize("x_first%d" % (2 * h + g), grouped, 1))
+                x_codes[s].extend(quantize("x_first%d" % g, grouped, 1))
 
         def first_pass(g):
             for n in range(2):
@@ -276,15 +284,12 @@ def tile_array_excitation_product_h1_kernel(
         nc.scalar.copy(out=taper[:].bitcast(F32), in_=spread[:])
         sort_x(0, 0)
         sort_x(0, 1)
-        first_half(0)
-        first_half(1)
+        by_pass(0)
         first_pass(0)
         first_pass(1)
         sort_x(1, 0)
         sort_x(1, 1)
-        xt = [turn_x(1, h) for h in range(2)]
-        x_grouped = [group_words(nc.scalar.copy, "x_grouped%d" % h, xt[h], 2) for h in range(2)]
-        x_codes[1] = quantize("x0", x_grouped[0], 2) + quantize("x1", x_grouped[1], 2)
+        by_pass(1)
         for n in range(2):
             for g in range(2, G1):
                 stage1_pass(0, n, g)
@@ -295,61 +300,95 @@ def tile_array_excitation_product_h1_kernel(
         stage1(1, 0)
 
         last = TILES - 1
-        for s in range(1, last):
+
+        def planes_half(s, n):
+            quantize_y(s, n, y_grouped[s][:, n * BANK:(n + 1) * BANK])
+            if n == 1:
+                store_planes(s)
+
+        def half_words(tag, name, pairs):
+            dst = bank(tag)
+            turn_pairs(dst, 0, pairs)
+            return group_words(nc.scalar.copy, name, dst, 1)
+
+        xt, h_half = [], []
+        for n in range(2):
+            xt.append(turn_x(2, n))
+            h_half.append(half_words(("ht", "yt")[n], "h_half%d" % n, h_pairs[0, n]))
+        taper_h(1, 0)
+        x_grouped = [group_words(nc.scalar.copy, "x_grouped%d" % h, xt[h], 2) for h in range(2)]
+        sort_x(3, 0)
+        sort_x(3, 1)
+        h_codes[0] = quantize("h_half0", h_half[0], 1) + quantize("h_half1", h_half[1], 1)
+        x_codes[2] = quantize("x0", x_grouped[0], 2) + quantize("x1", x_grouped[1], 2)
+        stage1(1, 1)
+        taper_h(1, 1)
+        for g in range(G2):
+            for n in range(2):
+                stage2_pass(0, n, g)
+        for n in range(2):
+            excite(0, n)
+        store_y(0, 0, F2)
+        stage1(2, 0)
+
+        for s in range(2, last):
             ht = turn_both("ht", h_pairs, s - 1)
             xt = [turn_x(s + 1, h) for h in range(2)]
-            if s >= 2:
-                yt = turn_both("yt", y_pairs, s - 2)
+            if s >= 3:
+                yt = turn_both("yt", y_pairs, s - 3)
             taper_h(s, 0)
             h_grouped = group_words(nc.scalar.copy, "h_grouped", ht, 2)
-            if s < last:
-                x_grouped = [group_words(nc.scalar.copy, "x_grouped%d" % h, xt[h], 2) for h in range(2)]
-            if s >= 2:
-                y_grouped = group_words(nc.scalar.copy, "y_grouped", yt, 2)
+            x_grouped = [group_words(nc.scalar.copy, "x_grouped%d" % h, xt[h], 2) for h in range(2)]
+            if s >= 3:
+                y_grouped[s - 3] = group_words(nc.scalar.copy, "y_grouped", yt, 2)
+            round_tile(s - 2)
             if s + 2 < TILES:
                 sort_x(s + 2, 0)
                 sort_x(s + 2, 1)
             h_codes[s - 1] = quantize("h", h_grouped, 2)
-            if s < last:
-                x_codes[s + 1] = quantize("x0", x_grouped[0], 2) + quantize("x1", x_grouped[1], 2)
+            if s >= 4:
+                planes_half(s - 4, 0)
+            x_codes[s + 1] = quantize("x0", x_grouped[0], 2)
+            if s >= 4:
+                planes_half(s - 4, 1)
+            x_codes[s + 1].extend(quantize("x1", x_grouped[1], 2))
             stage1(s, 1)
             taper_h(s, 1)
             stage2(s - 1)
             for n in range(2):
                 excite(s - 1, n)
-                round_y(s - 1, n)
             store_y(s - 1, 0, F2)
-            if s >= 2:
-                for n in range(2):
-                    quantize_y(s - 2, n, y_grouped[:, n * BANK:(n + 1) * BANK])
-                store_planes(s - 2)
-            if s < last:
-                stage1(s + 1, 0)
+            stage1(s + 1, 0)
 
         def last_h(n):
-            ht = bank(("xt0", "xt1")[n])
-            turn_pairs(ht, 0, h_pairs[last, n])
-            return group_words(nc.scalar.copy, "h_last%d" % n, ht, 1)
+            return quantize("h_half%d" % n, half_words("xt%d" % n, "h_half%d" % n, h_pairs[last, n]), 1)
 
-        def planes_of(s, grouped):
+        def turn_y(s, tag):
+            y_grouped[s] = group_words(nc.scalar.copy, "y_grouped", turn_both(tag, y_pairs, s), 2)
+
+        def planes(s):
             for n in range(2):
-                quantize_y(s, n, grouped[:, n * BANK:(n + 1) * BANK])
-            store_planes(s)
+                planes_half(s, n)
 
+        round_y(last - 2, 0)
         ht = turn_both("ht", h_pairs, last - 1)
+        yt = turn_both("yt", y_pairs, last - 3)
         taper_h(last, 0)
         h_grouped = group_words(nc.scalar.copy, "h_grouped", ht, 2)
+        round_y(last - 2, 1)
+        y_grouped[last - 3] = group_words(nc.scalar.copy, "y_grouped", yt, 2)
+        planes(last - 4)
         h_codes[last - 1] = quantize("h", h_grouped, 2)
         stage1(last, 1)
         taper_h(last, 1)
-        h_codes[last] = quantize("h_last0", last_h(0), 1)
+        planes(last - 3)
+        h_codes[last] = last_h(0)
+        turn_y(last - 2, "ht")
         for g in range(G2):
             stage2_pass(last - 1, 0, g)
         excite(last - 1, 0)
-        grouped = last_h(1)
-        yt = turn_both("yt", y_pairs, last - 2)
-        h_codes[last].extend(quantize("h_last1", grouped, 1))
-        y_grouped = group_words(nc.scalar.copy, "y_grouped", yt, 2)
+        planes_half(last - 2, 0)
+        h_codes[last].extend(last_h(1))
         round_y(last - 1, 0)
         for g in range(G2):
             stage2_pass(last - 1, 1, g)
@@ -359,21 +398,21 @@ def tile_array_excitation_product_h1_kernel(
         excite(last - 1, 1)
         round_y(last - 1, 1)
         store_y(last - 1, 0, F2)
-        planes_of(last - 2, y_grouped)
+        planes_half(last - 2, 1)
+        tail = {}
+        tail[last - 1, 0] = half_words("xt0", "y_half0", y_pairs[last - 1, 0])
         excite(last, 0)
         round_y(last, 0)
         store_y(last, 0, BANK)
         excite_pairs(last, 1)
         excite(last, 1)
         store_y(last, BANK, F2)
-        yt = turn_both("yt", y_pairs, last - 1)
-        y_grouped = group_words(nc.scalar.copy, "y_grouped", yt, 2)
-        tail = {}
+        tail[last - 1, 1] = half_words("xt1", "y_half1", y_pairs[last - 1, 1])
+        tail[last, 1] = half_words("ht", "y_half1", y_pairs[last, 1])
+        tail[last, 0] = half_words("yt", "y_half0", y_pairs[last, 0])
+        for n in range(2):
+            quantize_y(last - 1, n, tail[last - 1, n][:])
+        store_planes(last - 1)
         for n in (1, 0):
-            yt = bank(("xt0", "xt1")[n])
-            turn_pairs(yt, 0, y_pairs[last, n])
-            tail[n] = group_words((nc.scalar.copy, nc.vector.tensor_copy)[n], "y_last%d" % n, yt, 1)
-        planes_of(last - 1, y_grouped)
-        for n in (1, 0):
-            quantize_y(last, n, tail[n][:])
+            quantize_y(last, n, tail[last, n][:])
         store_planes(last)

@@ -21,7 +21,8 @@ BANK = 512
 TILES = T // P
 G1 = K1 // 512
 G2 = F2 // 512
-WORD_GROUPS = ((0, 3), (3, 5), (5, 7), (7, 8))
+SPLIT_TILES = 3
+WORD_GROUPS = ((0, 3), (3, 5), (5, 6), (6, 7), (7, 8))
 SCALE_GROUPS = ((0, 5), (5, 8))
 
 
@@ -45,59 +46,71 @@ def tile_array_excitation_product_h1_kernel(
         def rotating(tag, shape, dtype):
             return work.tile(shape, dtype, name=tag, tag=tag, align_bytes=64)
 
-        def load_scale_rows(plane, scales, passes):
+        def load_scale_rows(plane, scales):
             rows = scales.bitcast(I32).rearrange("g (q r) n -> r q g n", r=4)
             for r in range(4):
                 nc.sync.dma_start(
-                    out=plane[r:P:32, :].bitcast(I32).rearrange("q (g n) -> q g n", g=passes), in_=rows[r])
+                    out=plane[r:P:32, :].bitcast(I32).rearrange("q (g n) -> q g n", g=2), in_=rows[r])
 
-        s_scale = kept("s_scale", [P, G1 * F2], U8)
+        s_scale = [kept("s_scale%d" % h, [P, 2 * F2], U8) for h in range(2)]
         c_scale = kept("c_scale", [P, G2 * F2], U8)
-        nc.vector.memset(s_scale[:].bitcast(I32), 0)
+        nc.vector.memset(s_scale[0][:].bitcast(I32), 0)
         taper_col = kept("taper_col", [P, G2 * 4], BF16)
         nc.scalar.dma_start(
             out=taper_col[:].rearrange("p (g t) -> p g t", t=4),
             in_=conj_taper.rearrange("(g p t) -> p g t", p=P, t=4))
         ident = kept("ident", [P, P], F32)
         make_identity(nc, ident[:])
+        nc.vector.memset(s_scale[1][:].bitcast(I32), 0)
         nc.vector.memset(c_scale[:].bitcast(I32), 0)
 
         half = K1 // 2
-        x_first = [kept("x_first%d" % h, [P, half], BF16) for h in range(2)]
-        x_raw = [None] + [kept("x_raw%d" % s, [P, K1], BF16) for s in range(1, TILES)]
+        x_raw = {}
         s_words = [kept("s_words%d" % g, [P, 2 * F2], U8) for g in range(G1)]
         c_words = kept("c_words", [P, G2 * 2 * F2], U8)
-        exc = [kept("exc%d" % h, [P, TILES // 2, F], BF16) for h in range(2)]
+        exc = {}
         taper = kept("taper", [P, F2], BF16)
 
         def load_x(s):
-            nc.sync.dma_start(out=x_raw[s][:], in_=currents[s * P:(s + 1) * P, :])
+            rows = currents[s * P:(s + 1) * P, :]
+            if s < SPLIT_TILES:
+                for h in range(2):
+                    part = kept("x_raw%d_%d" % (s, h), [P, half], BF16)
+                    nc.sync.dma_start(out=part[:], in_=rows[:, h * half:(h + 1) * half])
+                    x_raw[s, h] = part[:].bitcast(F32)
+            else:
+                whole = kept("x_raw%d" % s, [P, K1], BF16)
+                nc.sync.dma_start(out=whole[:], in_=rows)
+                for h in range(2):
+                    x_raw[s, h] = whole[:].bitcast(F32)[:, h * BANK:(h + 1) * BANK]
 
         def load_s(g):
             nc.sync.dma_start(out=s_words[g][:].bitcast(I32), in_=steering_words[g].bitcast(I32))
 
-        def load_exc(h):
-            rows = excitation[h * T // 2:(h + 1) * T // 2, :]
-            nc.sync.dma_start(out=exc[h][:], in_=rows.rearrange("(s p) j -> p s j", p=P))
+        def load_exc(lo, hi):
+            group = kept("exc%d" % lo, [P, hi - lo, F], BF16)
+            nc.sync.dma_start(out=group[:], in_=excitation[lo * P:hi * P, :].rearrange("(s p) j -> p s j", p=P))
+            for s in range(lo, hi):
+                exc[s] = group[:, s - lo, :]
 
-        nc.sync.dma_start(out=x_first[0][:], in_=currents[0:P, 0:half])
-        nc.sync.dma_start(out=x_first[1][:], in_=currents[0:P, half:K1])
-        load_scale_rows(s_scale, steering_scales, G1)
+        load_x(0)
+        load_scale_rows(s_scale[0], steering_scales[0:2])
         load_s(0)
         load_s(1)
         load_x(1)
+        load_scale_rows(s_scale[1], steering_scales[2:4])
         load_s(2)
         load_s(3)
         load_x(2)
-        load_scale_rows(c_scale, coupling_scales, G2)
+        load_scale_rows(c_scale, coupling_scales)
         nc.sync.dma_start(
             out=c_words[:].bitcast(I32).rearrange("p (g n) -> p g n", g=G2),
             in_=coupling_words.bitcast(I32).rearrange("g p n -> p g n"))
         load_x(3)
-        load_exc(0)
+        load_exc(0, 2)
         load_x(4)
         load_x(5)
-        load_exc(1)
+        load_exc(2, TILES)
         load_x(6)
         load_x(7)
 
@@ -117,10 +130,7 @@ def tile_array_excitation_product_h1_kernel(
 
         def sort_x(s, h):
             dst = rotating("x_sorted%d" % h, [P, BANK], F32)
-            if s == 0:
-                src = x_first[h][:].bitcast(F32)
-            else:
-                src = x_raw[s][:].bitcast(F32)[:, h * BANK:(h + 1) * BANK]
+            src = x_raw[s, h]
             out = dst[:].rearrange("p (u c i) -> p c u i", u=2, i=4)
             in_ = src.rearrange("p (c i u) -> p c u i", u=2, i=4)
             if s <= 1 or (h == 0 and s > 2):
@@ -170,7 +180,7 @@ def tile_array_excitation_product_h1_kernel(
         def stage1_pass(s, n, g):
             if g == 0:
                 h_bank[s, n] = bank(("y%d" if s == 0 else "h%d") % n)
-            mx_pass(h_bank[s, n], x_codes[s][g], s_words[g][:], s_scale[:, g * F2:(g + 1) * F2], n,
+            mx_pass(h_bank[s, n], x_codes[s][g], s_words[g][:], s_scale[g // 2][:, (g % 2) * F2:(g % 2 + 1) * F2], n,
                     g == 0, g == G1 - 1)
 
         def stage1(s, n):
@@ -202,7 +212,7 @@ def tile_array_excitation_product_h1_kernel(
                 y_f32[s] = rotating("y_f32", [P, F2], F32)
             nc.vector.scalar_tensor_tensor(
                 out=y_f32[s][:, n * BANK:(n + 1) * BANK], in0=y_bank[s, n][:], scalar=NORM,
-                in1=exc[s // (TILES // 2)][:, s % (TILES // 2), :], op0=MULT, op1=MULT)
+                in1=exc[s], op0=MULT, op1=MULT)
 
         def round_y(s, n):
             dst = rotating("y_pairs%d" % n, [P, BANK], BF16)
@@ -221,7 +231,7 @@ def tile_array_excitation_product_h1_kernel(
 
         def excite_pairs(s, n):
             dst = rotating("y_pairs%d" % n, [P, BANK], BF16)
-            factor = exc[s // (TILES // 2)][:, s % (TILES // 2), :]
+            factor = exc[s]
             for u in range(2):
                 nc.vector.scalar_tensor_tensor(
                     out=dst[:, u * 2 * P:(u + 1) * 2 * P].rearrange("p (w e) -> p w e", e=2),
@@ -269,8 +279,11 @@ def tile_array_excitation_product_h1_kernel(
             for g in range(G1):
                 dst = bank(first_tags[g])
                 for u in range(2):
-                    start = u * 2 * P + (g % 2) * P
-                    turn(dst, u, x_sorted[s, g // 2][:, start:start + P])
+                    if (s, g // 2) in x_sorted:
+                        start = u * 2 * P + (g % 2) * P
+                        turn(dst, u, x_sorted[s, g // 2][:, start:start + P])
+                    else:
+                        turn(dst, u, x_raw[0, 0][:, g * 2 * P + u:(g + 1) * 2 * P:2])
                 grouped = group_words(nc.scalar.copy, "x_first_grouped", dst, 1)
                 x_codes[s].extend(quantize("x_first%d" % g, grouped, 1))
 
@@ -282,7 +295,6 @@ def tile_array_excitation_product_h1_kernel(
         for slot in range(4):
             turn(spread, slot, taper_col[:].bitcast(F32)[:, slot:slot + 1].to_broadcast([P, P]))
         nc.scalar.copy(out=taper[:].bitcast(F32), in_=spread[:])
-        sort_x(0, 0)
         sort_x(0, 1)
         by_pass(0)
         first_pass(0)
@@ -290,9 +302,8 @@ def tile_array_excitation_product_h1_kernel(
         sort_x(1, 0)
         sort_x(1, 1)
         by_pass(1)
-        for n in range(2):
-            for g in range(2, G1):
-                stage1_pass(0, n, g)
+        first_pass(2)
+        first_pass(3)
         sort_x(2, 0)
         sort_x(2, 1)
         taper_h(0, 0)
@@ -317,10 +328,11 @@ def tile_array_excitation_product_h1_kernel(
             h_half.append(half_words(("ht", "yt")[n], "h_half%d" % n, h_pairs[0, n]))
         taper_h(1, 0)
         x_grouped = [group_words(nc.scalar.copy, "x_grouped%d" % h, xt[h], 2) for h in range(2)]
+        h_codes[0] = quantize("h_half0", h_half[0], 1) + quantize("h_half1", h_half[1], 1)
+        x_codes[2] = quantize("x0", x_grouped[0], 2)
         sort_x(3, 0)
         sort_x(3, 1)
-        h_codes[0] = quantize("h_half0", h_half[0], 1) + quantize("h_half1", h_half[1], 1)
-        x_codes[2] = quantize("x0", x_grouped[0], 2) + quantize("x1", x_grouped[1], 2)
+        x_codes[2].extend(quantize("x1", x_grouped[1], 2))
         stage1(1, 1)
         taper_h(1, 1)
         for g in range(G2):

from contextlib import ExitStack

import concourse.mybir as mybir
from concourse.masks import make_identity

T, K1, F2, F = 1024, 2048, 1024, 512
NORM = 0.75
FLOPS = 2 * T * K1 * F2 + 2 * T * F2 * F2

F32 = mybir.dt.float32
BF16 = mybir.dt.bfloat16
I32 = mybir.dt.int32
U32 = mybir.dt.uint32
U8 = mybir.dt.uint8
FP8X4 = mybir.dt.float8_e4m3fn_x4
FP4X4 = mybir.dt.float4_e2m1fn_x4
MULT = mybir.AluOpType.mult

P = 128
BANK = 512
TILES = T // P
G1 = K1 // 512
G2 = F2 // 512
SPLIT_TILES = 3
WORD_GROUPS = ((0, 3), (3, 5), (5, 6), (6, 7), (7, 8))
SCALE_GROUPS = ((0, 5), (5, 8))


def tile_array_excitation_product_h1_kernel(
    tc, currents, steering_words, steering_scales, conj_taper, coupling_words, coupling_scales, excitation,
    out_0, out_1, out_2,
):
    nc = tc.nc
    with ExitStack() as ctx:
        keep = ctx.enter_context(tc.tile_pool(name="keep", bufs=1))
        work = ctx.enter_context(tc.tile_pool(name="work", bufs=3))
        psum = ctx.enter_context(tc.psum_pool(name="psum", bufs=1))
        ctx.enter_context(tc.manual_schedule())

        def bank(tag):
            return psum.tile([P, BANK], F32, name=tag, tag=tag)

        def kept(name, shape, dtype):
            return keep.tile(shape, dtype, name=name, tag=name, align_bytes=64)

        def rotating(tag, shape, dtype):
            return work.tile(shape, dtype, name=tag, tag=tag, align_bytes=64)

        def load_scale_rows(plane, scales):
            rows = scales.bitcast(I32).rearrange("g (q r) n -> r q g n", r=4)
            for r in range(4):
                nc.sync.dma_start(
                    out=plane[r:P:32, :].bitcast(I32).rearrange("q (g n) -> q g n", g=2), in_=rows[r])

        s_scale = [kept("s_scale%d" % h, [P, 2 * F2], U8) for h in range(2)]
        c_scale = kept("c_scale", [P, G2 * F2], U8)
        nc.vector.memset(s_scale[0][:].bitcast(I32), 0)
        taper_col = kept("taper_col", [P, G2 * 4], BF16)
        nc.scalar.dma_start(
            out=taper_col[:].rearrange("p (g t) -> p g t", t=4),
            in_=conj_taper.rearrange("(g p t) -> p g t", p=P, t=4))
        ident = kept("ident", [P, P], F32)
        make_identity(nc, ident[:])
        nc.vector.memset(s_scale[1][:].bitcast(I32), 0)
        nc.vector.memset(c_scale[:].bitcast(I32), 0)

        half = K1 // 2
        x_raw = {}
        s_words = [kept("s_words%d" % g, [P, 2 * F2], U8) for g in range(G1)]
        c_words = kept("c_words", [P, G2 * 2 * F2], U8)
        exc = {}
        taper = kept("taper", [P, F2], BF16)

        def load_x(s):
            rows = currents[s * P:(s + 1) * P, :]
            if s < SPLIT_TILES:
                for h in range(2):
                    part = kept("x_raw%d_%d" % (s, h), [P, half], BF16)
                    nc.sync.dma_start(out=part[:], in_=rows[:, h * half:(h + 1) * half])
                    x_raw[s, h] = part[:].bitcast(F32)
            else:
                whole = kept("x_raw%d" % s, [P, K1], BF16)
                nc.sync.dma_start(out=whole[:], in_=rows)
                for h in range(2):
                    x_raw[s, h] = whole[:].bitcast(F32)[:, h * BANK:(h + 1) * BANK]

        def load_s(g):
            nc.sync.dma_start(out=s_words[g][:].bitcast(I32), in_=steering_words[g].bitcast(I32))

        def load_exc(lo, hi):
            group = kept("exc%d" % lo, [P, hi - lo, F], BF16)
            nc.sync.dma_start(out=group[:], in_=excitation[lo * P:hi * P, :].rearrange("(s p) j -> p s j", p=P))
            for s in range(lo, hi):
                exc[s] = group[:, s - lo, :]

        load_x(0)
        load_scale_rows(s_scale[0], steering_scales[0:2])
        load_s(0)
        load_s(1)
        load_x(1)
        load_scale_rows(s_scale[1], steering_scales[2:4])
        load_s(2)
        load_s(3)
        load_x(2)
        load_scale_rows(c_scale, coupling_scales)
        nc.sync.dma_start(
            out=c_words[:].bitcast(I32).rearrange("p (g n) -> p g n", g=G2),
            in_=coupling_words.bitcast(I32).rearrange("g p n -> p g n"))
        load_x(3)
        load_exc(0, 2)
        load_x(4)
        load_x(5)
        load_exc(2, TILES)
        load_x(6)
        load_x(7)

        y_words = {}
        for lo, hi in WORD_GROUPS:
            group = kept("y_words%d" % lo, [P, G2, (hi - lo) * P], U32)
            for s in range(lo, hi):
                y_words[s] = (group, lo, hi)
        y_scale = {}
        for lo, hi in SCALE_GROUPS:
            group = kept("y_scale%d" % lo, [P, G2, (hi - lo) * P], U8)
            for s in range(lo, hi):
                y_scale[s] = (group, lo, hi)

        x_sorted, x_codes, h_bank, h_pairs, h_codes = {}, {}, {}, {}, {}
        y_bank, y_f32, y_pairs, y_grouped = {}, {}, {}, {}

        def sort_x(s, h):
            dst = rotating("x_sorted%d" % h, [P, BANK], F32)
            src = x_raw[s, h]
            out = dst[:].rearrange("p (u c i) -> p c u i", u=2, i=4)
            in_ = src.rearrange("p (c i u) -> p c u i", u=2, i=4)
            if s <= 1 or (h == 0 and s > 2):
                nc.vector.tensor_copy(out=out, in_=in_)
            else:
                nc.scalar.copy(out=out, in_=in_)
            x_sorted[s, h] = dst

        def turn(dst, slot, words):
            nc.tensor.transpose(dst[:, slot * P:(slot + 1) * P], words, ident[:])

        def turn_x(s, h):
            dst = bank("xt%d" % h)
            for g in range(2):
                for u in range(2):
                    start = u * 2 * P + g * P
                    turn(dst, 2 * g + u, x_sorted[s, h][:, start:start + P])
            return dst

        def turn_pairs(dst, first_slot, pairs):
            words = pairs[:].bitcast(F32)
            for u in range(2):
                turn(dst, first_slot + u, words[:, u * P:(u + 1) * P])

        def group_words(engine_copy, tag, src, passes):
            dst = rotating(tag, [P, passes * BANK], BF16)
            engine_copy(
                out=dst[:].bitcast(F32).rearrange("p (g r u) -> p g r u", g=passes, u=2),
                in_=src[:, 0:passes * 2 * P].rearrange("p (g u r) -> p g r u", g=passes, u=2))
            return dst

        def quantize(tag, grouped, passes):
            codes = rotating(tag + "_codes", [P, passes * P], U32)
            scales = rotating(tag + "_scales", [P, passes * P], U8)
            nc.vector.quantize_mx(out=codes[:].bitcast(FP8X4), scales=scales[:], in_=grouped[:])
            return [(codes[:, g * P:(g + 1) * P], scales[:, g * P:(g + 1) * P]) for g in range(passes)]

        def mx_pass(acc, stationary, words, scale, n, first, last):
            codes, scales = stationary
            nc.tensor.matmul_mx(
                out=acc[:],
                lhsT=codes.bitcast(FP8X4), lhsT_scale=scales,
                rhs=words[:, n * 2 * BANK:(n + 1) * 2 * BANK].bitcast(FP4X4),
                rhs_scale=scale[:, n * BANK:(n + 1) * BANK],
                start=first, stop=last)

        def stage1_pass(s, n, g):
            if g == 0:
                h_bank[s, n] = bank(("y%d" if s == 0 else "h%d") % n)
            mx_pass(h_bank[s, n], x_codes[s][g], s_words[g][:], s_scale[g // 2][:, (g % 2) * F2:(g % 2 + 1) * F2], n,
                    g == 0, g == G1 - 1)

        def stage1(s, n):
            for g in range(G1):
                stage1_pass(s, n, g)

        def stage2_pass(s, n, g):
            if g == 0:
                y_bank[s, n] = bank(("h%d" if s == TILES - 1 else "y%d") % n)
            mx_pass(y_bank[s, n], h_codes[s][g], c_words[:, g * 2 * F2:(g + 1) * 2 * F2],
                    c_scale[:, g * F2:(g + 1) * F2], n, g == 0, g == G2 - 1)

        def stage2(s):
            for n in range(2):
                for g in range(G2):
                    stage2_pass(s, n, g)

        def taper_h(s, n):
            dst = rotating("h_pairs%d" % n, [P, BANK], BF16)
            nc.vector.tensor_tensor(
                out=dst[:].rearrange("p (u w e) -> p u w e", u=2, e=2),
                in0=h_bank[s, n][:].rearrange("p (w u e) -> p u w e", u=2, e=2),
                in1=taper[:, n * BANK:(n + 1) * BANK].rearrange("p (u w e) -> p u w e", u=2, e=2),
                op=MULT)
            h_pairs[s, n] = dst

        def excite(s, n):
            if n == 0:
                y_f32[s] = rotating("y_f32", [P, F2], F32)
            nc.vector.scalar_tensor_tensor(
                out=y_f32[s][:, n * BANK:(n + 1) * BANK], in0=y_bank[s, n][:], scalar=NORM,
                in1=exc[s], op0=MULT, op1=MULT)

        def round_y(s, n):
            dst = rotating("y_pairs%d" % n, [P, BANK], BF16)
            nc.scalar.copy(
                out=dst[:].rearrange("p (u w e) -> p u w e", u=2, e=2),
                in_=y_f32[s][:, n * BANK:(n + 1) * BANK].rearrange("p (w u e) -> p u w e", u=2, e=2))
            y_pairs[s, n] = dst

        def round_tile(s):
            dst = rotating("y_pairs", [P, F2], BF16)
            nc.scalar.copy(
                out=dst[:].rearrange("p (g u w e) -> p g u w e", g=G2, u=2, e=2),
                in_=y_f32[s][:].rearrange("p (g w u e) -> p g u w e", g=G2, u=2, e=2))
            for n in range(2):
                y_pairs[s, n] = dst[:, n * BANK:(n + 1) * BANK]

        def excite_pairs(s, n):
            dst = rotating("y_pairs%d" % n, [P, BANK], BF16)
            factor = exc[s]
            for u in range(2):
                nc.vector.scalar_tensor_tensor(
                    out=dst[:, u * 2 * P:(u + 1) * 2 * P].rearrange("p (w e) -> p w e", e=2),
                    in0=y_bank[s, n][:].rearrange("p (w u e) -> p u w e", u=2, e=2)[:, u],
                    scalar=NORM,
                    in1=factor.rearrange("p (w u e) -> p u w e", u=2, e=2)[:, u],
                    op0=MULT, op1=MULT)
            y_pairs[s, n] = dst

        def quantize_y(s, n, grouped):
            words, wlo, whi = y_words[s]
            scales, slo, shi = y_scale[s]
            nc.vector.quantize_mx(
                out=words[:, n, (s - wlo) * P:(s - wlo + 1) * P].bitcast(FP8X4),
                scales=scales[:, n, (s - slo) * P:(s - slo + 1) * P],
                in_=grouped)

        def store_y(s, lo, hi):
            nc.sync.dma_start(out=out_0[s * P:(s + 1) * P, lo:hi], in_=y_f32[s][:, lo:hi])

        def store_planes(s):
            words, wlo, whi = y_words[s]
            if s == whi - 1:
                dst = out_1.rearrange("g p m t -> p g (m t)").bitcast(I32)
                nc.sync.dma_start(out=dst[:, :, wlo * P:whi * P], in_=words[:].bitcast(I32))
            scales, slo, shi = y_scale[s]
            if s == shi - 1:
                dst = out_2.bitcast(I32).rearrange("g q m -> q g m")
                for q in range(4):
                    queue = nc.scalar if (s == TILES - 1 and q % 2 == 1) else nc.sync
                    queue.dma_start(
                        out=dst[4 * q:4 * q + 4, :, slo * P // 4:shi * P // 4],
                        in_=scales[32 * q:32 * q + 4, :, :].bitcast(I32))

        def turn_both(tag, pairs, s):
            dst = bank(tag)
            for n in range(2):
                turn_pairs(dst, 2 * n, pairs[s, n])
            return dst

        first_tags = ("xt0", "xt1", "ht", "yt")

        def by_pass(s):
            x_codes[s] = []
            for g in range(G1):
                dst = bank(first_tags[g])
                for u in range(2):
                    if (s, g // 2) in x_sorted:
                        start = u * 2 * P + (g % 2) * P
                        turn(dst, u, x_sorted[s, g // 2][:, start:start + P])
                    else:
                        turn(dst, u, x_raw[0, 0][:, g * 2 * P + u:(g + 1) * 2 * P:2])
                grouped = group_words(nc.scalar.copy, "x_first_grouped", dst, 1)
                x_codes[s].extend(quantize("x_first%d" % g, grouped, 1))

        def first_pass(g):
            for n in range(2):
                stage1_pass(0, n, g)

        spread = bank("h1")
        for slot in range(4):
            turn(spread, slot, taper_col[:].bitcast(F32)[:, slot:slot + 1].to_broadcast([P, P]))
        nc.scalar.copy(out=taper[:].bitcast(F32), in_=spread[:])
        sort_x(0, 1)
        by_pass(0)
        first_pass(0)
        first_pass(1)
        sort_x(1, 0)
        sort_x(1, 1)
        by_pass(1)
        first_pass(2)
        first_pass(3)
        sort_x(2, 0)
        sort_x(2, 1)
        taper_h(0, 0)
        taper_h(0, 1)
        stage1(1, 0)

        last = TILES - 1

        def planes_half(s, n):
            quantize_y(s, n, y_grouped[s][:, n * BANK:(n + 1) * BANK])
            if n == 1:
                store_planes(s)

        def half_words(tag, name, pairs):
            dst = bank(tag)
            turn_pairs(dst, 0, pairs)
            return group_words(nc.scalar.copy, name, dst, 1)

        xt, h_half = [], []
        for n in range(2):
            xt.append(turn_x(2, n))
            h_half.append(half_words(("ht", "yt")[n], "h_half%d" % n, h_pairs[0, n]))
        taper_h(1, 0)
        x_grouped = [group_words(nc.scalar.copy, "x_grouped%d" % h, xt[h], 2) for h in range(2)]
        h_codes[0] = quantize("h_half0", h_half[0], 1) + quantize("h_half1", h_half[1], 1)
        x_codes[2] = quantize("x0", x_grouped[0], 2)
        sort_x(3, 0)
        sort_x(3, 1)
        x_codes[2].extend(quantize("x1", x_grouped[1], 2))
        stage1(1, 1)
        taper_h(1, 1)
        for g in range(G2):
            for n in range(2):
                stage2_pass(0, n, g)
        for n in range(2):
            excite(0, n)
        store_y(0, 0, F2)
        stage1(2, 0)

        for s in range(2, last):
            ht = turn_both("ht", h_pairs, s - 1)
            xt = [turn_x(s + 1, h) for h in range(2)]
            if s >= 3:
                yt = turn_both("yt", y_pairs, s - 3)
            taper_h(s, 0)
            h_grouped = group_words(nc.scalar.copy, "h_grouped", ht, 2)
            x_grouped = [group_words(nc.scalar.copy, "x_grouped%d" % h, xt[h], 2) for h in range(2)]
            if s >= 3:
                y_grouped[s - 3] = group_words(nc.scalar.copy, "y_grouped", yt, 2)
            round_tile(s - 2)
            if s + 2 < TILES:
                sort_x(s + 2, 0)
                sort_x(s + 2, 1)
            h_codes[s - 1] = quantize("h", h_grouped, 2)
            if s >= 4:
                planes_half(s - 4, 0)
            x_codes[s + 1] = quantize("x0", x_grouped[0], 2)
            if s >= 4:
                planes_half(s - 4, 1)
            x_codes[s + 1].extend(quantize("x1", x_grouped[1], 2))
            stage1(s, 1)
            taper_h(s, 1)
            stage2(s - 1)
            for n in range(2):
                excite(s - 1, n)
            store_y(s - 1, 0, F2)
            stage1(s + 1, 0)

        def last_h(n):
            return quantize("h_half%d" % n, half_words("xt%d" % n, "h_half%d" % n, h_pairs[last, n]), 1)

        def turn_y(s, tag):
            y_grouped[s] = group_words(nc.scalar.copy, "y_grouped", turn_both(tag, y_pairs, s), 2)

        def planes(s):
            for n in range(2):
                planes_half(s, n)

        round_y(last - 2, 0)
        ht = turn_both("ht", h_pairs, last - 1)
        yt = turn_both("yt", y_pairs, last - 3)
        taper_h(last, 0)
        h_grouped = group_words(nc.scalar.copy, "h_grouped", ht, 2)
        round_y(last - 2, 1)
        y_grouped[last - 3] = group_words(nc.scalar.copy, "y_grouped", yt, 2)
        planes(last - 4)
        h_codes[last - 1] = quantize("h", h_grouped, 2)
        stage1(last, 1)
        taper_h(last, 1)
        planes(last - 3)
        h_codes[last] = last_h(0)
        turn_y(last - 2, "ht")
        for g in range(G2):
            stage2_pass(last - 1, 0, g)
        excite(last - 1, 0)
        planes_half(last - 2, 0)
        h_codes[last].extend(last_h(1))
        round_y(last - 1, 0)
        for g in range(G2):
            stage2_pass(last - 1, 1, g)
        for g in range(G2):
            for n in range(2):
                stage2_pass(last, n, g)
        excite(last - 1, 1)
        round_y(last - 1, 1)
        store_y(last - 1, 0, F2)
        planes_half(last - 2, 1)
        tail = {}
        tail[last - 1, 0] = half_words("xt0", "y_half0", y_pairs[last - 1, 0])
        excite(last, 0)
        round_y(last, 0)
        store_y(last, 0, BANK)
        excite_pairs(last, 1)
        excite(last, 1)
        store_y(last, BANK, F2)
        tail[last - 1, 1] = half_words("xt1", "y_half1", y_pairs[last - 1, 1])
        tail[last, 1] = half_words("ht", "y_half1", y_pairs[last, 1])
        tail[last, 0] = half_words("yt", "y_half0", y_pairs[last, 0])
        for n in range(2):
            quantize_y(last - 1, n, tail[last - 1, n][:])
        store_planes(last - 1)
        for n in (1, 0):
            quantize_y(last, n, tail[last, n][:])
        store_planes(last)
